import numpy as np
import ml_dtypes


def mxq(x, axis, fmt="e4m3"):
    dtype, down = {"e4m3": (ml_dtypes.float8_e4m3fn, 7), "e5m2": (ml_dtypes.float8_e5m2, 14)}[fmt]
    v = np.moveaxis(np.asarray(x, np.float32).astype(ml_dtypes.bfloat16).astype(np.float64), axis, -1)
    blocks = v.reshape(v.shape[:-1] + (-1, 32))
    amax = np.abs(blocks).max(-1, keepdims=True)
    byte = np.maximum(np.where(amax > 0, np.frexp(amax)[1] - 1 + 127, 0) - down, 1)
    scale = np.exp2(byte - 127.0)
    codes = (blocks / scale).astype(np.float32).astype(dtype).astype(np.float64)
    return np.moveaxis((codes * scale).reshape(v.shape), -1, axis)


WIDE = False


def mx_kscale(k):
    if not WIDE:
        return np.ones(k)
    levels = np.array([10, -10, 5, -5, 0])
    if k % 512:
        return np.exp2(np.random.permutation(np.resize(levels, k // 32))).repeat(32)
    a = np.empty((k // 512, 16))
    for p in range(k // 512):
        a[p, :8] = np.random.permutation(np.resize(levels, 8))
        for g in range(8):
            far = levels[np.abs(levels - a[p, g]) >= 10]
            a[p, g + 8] = far[np.random.randint(len(far))]
    return np.exp2(a.ravel()).repeat(32)


def f64(x):
    return np.asarray(x).astype(np.float64)


def striped8(idx):
    return np.asarray(idx).reshape(8, -1, 16).transpose(0, 2, 1).reshape(128, -1).astype(np.uint16)


def unstriped8(offs):
    return offs.reshape(8, 16, -1).transpose(0, 2, 1).reshape(8, -1).astype(np.int64)


def pick8(x, idx, run):
    r = np.arange(len(x))
    return x[r[:, None], idx[r % (8 * run) // run]]


E2M1 = np.array([0.0, 0.5, 1.0, 1.5, 2.0, 3.0, 4.0, 6.0, -0.0, -0.5, -1.0, -1.5, -2.0, -3.0, -4.0, -6.0])


def pack_weight(w, fmt):
    k, n = w.shape
    w = f64(np.asarray(w, np.float32).astype(ml_dtypes.bfloat16)).reshape(k // 32, 32, n)
    amax = np.abs(w).max(1)
    if fmt == "e4m3":
        byte = np.frexp(amax)[1] - 1 + 127 - 7
    else:
        mant, ex = np.frexp(amax / 6.0)
        byte = np.where(mant > 0.5, ex, ex - 1) + 127
    byte = np.clip(np.where(amax > 0, byte, 1), 1, 254)
    scaled = (w * np.exp2(127.0 - byte)[:, None, :]).reshape(k, n).astype(np.float32)
    by_word = np.ascontiguousarray(scaled.reshape(k // 512, 128, 4, n).transpose(0, 1, 3, 2))
    if fmt == "e4m3":
        words = by_word.astype(ml_dtypes.float8_e4m3fn).view(np.uint8)
    else:
        c = by_word.astype(ml_dtypes.float4_e2m1fn).view(np.uint8) & 0xF
        words = (c[..., 0::2] | (c[..., 1::2] << 4)).reshape(k // 512, 128, 2 * n)
    return np.ascontiguousarray(words), np.ascontiguousarray(byte.astype(np.uint8).reshape(k // 512, 16, n))


def unpack_weight(words, scales, fmt):
    g, _, n = scales.shape
    words = np.ascontiguousarray(words).reshape(g, 128, n, -1)
    if fmt == "e4m3":
        vals = words.view(ml_dtypes.float8_e4m3fn).astype(np.float64)
    else:
        nib = np.empty((g, 128, n, 4), np.uint8)
        nib[..., 0::2] = words & 0xF
        nib[..., 1::2] = words >> 4
        vals = E2M1[nib]
    vals = vals * np.repeat(np.exp2(scales.astype(np.float64) - 127.0), 8, axis=1)[..., None]
    return vals.transpose(0, 1, 3, 2).reshape(g * 512, n)


D, T, Q, I, E = 512, 1024, 128, 256, 512


def setup_inputs():
    n = np.random.standard_normal
    idx = np.stack([np.random.permutation(T)[:I] for _ in range(8)])
    fd = mx_kscale(D)
    ft = mx_kscale(T)
    keysp = pack_weight(n((D, T)) / fd[:, None], "e2m1")
    return {
        "query": (n((D, Q)) * 0.5 / np.sqrt(D) * fd[:, None]).astype(np.float32),
        "keys_words": keysp[0],
        "keys_scales": keysp[1],
        "fac": (np.random.uniform(16.0, 64.0, (1, T)) * ft).astype(np.float32),
        "vals": (n((T, E)) / ft[:, None]).astype(np.float32),
        "offs": striped8(idx),
    }


def reference(query, keys_words, keys_scales, fac, vals, offs):
    idx = unstriped8(offs)
    keysu = unpack_weight(keys_words, keys_scales, "e2m1")
    queryq = mxq(f64(query), 0, "e4m3")
    a = queryq.T @ keysu
    m1 = np.max(a, axis=1, keepdims=True)
    p = np.exp(a - m1)
    pk = np.exp(pick8(a, idx, 16) - m1)
    pf = np.zeros((Q, T))
    pf[np.arange(Q)[:, None], idx[np.arange(Q) % 128 // 16]] = pk
    z = np.sum(p, axis=1, keepdims=True)
    z2 = z - np.sum(pk, axis=1, keepdims=True)
    w = (p / z - (p - pf) / z2) * f64(fac)
    wt = w.T
    wtq = mxq(wt, 0, "e4m3")
    valsq = mxq(f64(vals), 0, "e4m3")
    o = wtq.T @ valsq
    return o

@@ -1,0 +1,241 @@
+from contextlib import ExitStack
+
+import concourse.mybir as mybir
+from concourse.masks import make_identity
+
+D, T, Q, I, E = 512, 1024, 128, 256, 512
+FLOPS = 2 * D * Q * T + 2 * T * Q * E
+
+F32 = mybir.dt.float32
+BF16 = mybir.dt.bfloat16
+U32 = mybir.dt.uint32
+I32 = mybir.dt.int32
+U16 = mybir.dt.uint16
+U8 = mybir.dt.uint8
+FP8X4 = mybir.dt.float8_e4m3fn_x4
+FP4X4 = mybir.dt.float4_e2m1fn_x4
+ALU = mybir.AluOpType
+ACT = mybir.ActivationFunctionType
+AX = mybir.AxisListType
+
+P = 128
+PACK = 4
+KP = P * PACK
+PASSES = T // KP
+HALF = E // 2
+PIECE = 128
+
+
+def interleave(eng, nc, dst, src):
+    d = dst.rearrange("p (c i) t -> p c t i", i=4)
+    s = src.rearrange("p t (c i) -> p c t i", i=4)
+    if eng == "S":
+        nc.scalar.copy(out=d, in_=s)
+    elif eng == "V":
+        nc.vector.tensor_copy(out=d, in_=s)
+    else:
+        nc.gpsimd.tensor_scalar(out=d, in0=s, scalar1=1.0, scalar2=0.0, op0=ALU.mult, op1=ALU.add)
+
+
+def tile_attend_knockout_heads_kernel(tc, query, keys_words, keys_scales, fac, vals, offs, out):
+    nc = tc.nc
+    with ExitStack() as ctx:
+        sb = ctx.enter_context(tc.tile_pool(name="sb", bufs=1))
+        ps = ctx.enter_context(tc.psum_pool(name="ps", bufs=1))
+
+        def tile(shape, dtype, name, tag=None):
+            return sb.tile(shape, dtype, name=name, tag=tag or name, align_bytes=64)
+
+        offsets = sb.tile([P, I // 16], U16, name="offsets")
+        k_scales = tile([P, T], U8, "k_scales")
+        nc.vector.memset(k_scales[:].bitcast(I32), 0)
+        warm_in = tile([P, 1], F32, "warm_in")
+        nc.vector.memset(warm_in[:], 0.0)
+        warm_out = tile([P, 1], F32, "warm_out")
+        nc.scalar.activation(out=warm_out[:], in_=warm_in[:], func=ACT.Exp)
+
+        q_raw = tile([P, PACK, Q], F32, "q_raw")
+        nc.sync.dma_start(out=q_raw[:], in_=query.rearrange("(p j) q -> p j q", j=PACK))
+        k_words = tile([P, 2 * T], U8, "k_words")
+        nc.sync.dma_start(out=k_words[:].bitcast(I32), in_=keys_words[0].bitcast(I32))
+        for quad in range(4):
+            nc.sync.dma_start(
+                out=k_scales[32 * quad : 32 * quad + 4, :].bitcast(I32),
+                in_=keys_scales[0, 4 * quad : 4 * quad + 4, :].bitcast(I32),
+            )
+        v_raw = {}
+
+        def load_vals(g, h):
+            t = tile([P, PACK, HALF], F32, f"v_raw{g}{h}")
+            rows = vals[g * KP : (g + 1) * KP, h * HALF : (h + 1) * HALF]
+            nc.sync.dma_start(out=t[:], in_=rows.rearrange("(p j) e -> p j e", j=PACK))
+            v_raw[g, h] = t
+
+        load_vals(0, 0)
+        load_vals(0, 1)
+        nc.sync.dma_start(offsets[:], offs)
+        load_vals(1, 0)
+        load_vals(1, 1)
+        fac_t = tile([P, PASSES, PACK], F32, "fac_t")
+        nc.sync.dma_start(out=fac_t[:], in_=fac[0].rearrange("(g p j) -> p g j", p=P, j=PACK))
+
+        ident = tile([P, P], F32, "ident")
+        make_identity(nc, ident[:])
+        pf = tile([P, T], F32, "pf")
+        nc.vector.memset(pf[:], 0.0)
+
+        v_bf = {}
+        v_codes = {}
+        v_scales = {}
+
+        def cast(piece, eng, tag=None):
+            g, h, c0 = piece // 4, piece // 2 % 2, piece % 2 * PIECE
+            if piece == 4:
+                late = tile([P, 4, PIECE, PACK], BF16, "v_bf_late", tag)
+                for i in range(4):
+                    v_bf[4 + i] = late[:, i]
+            elif piece < 4:
+                v_bf[piece] = tile([P, PIECE, PACK], BF16, f"v_bf{piece}", tag)[:]
+            interleave(eng, nc, v_bf[piece], v_raw[g, h][:, :, c0 : c0 + PIECE])
+
+        def quant(piece, tag=None):
+            g, h, c0 = piece // 4, piece // 2 % 2, piece % 2 * PIECE
+            if (g, h) not in v_codes:
+                v_codes[g, h] = tile([P, HALF], U32, f"v_codes{g}{h}", tag)
+                v_scales[g, h] = tile([P, HALF], U8, f"v_scales{g}{h}")
+            nc.vector.quantize_mx(
+                out=v_codes[g, h][:, c0 : c0 + PIECE].bitcast(FP8X4), scales=v_scales[g, h][:, c0 : c0 + PIECE],
+                in_=v_bf[piece].rearrange("p e j -> p (e j)"),
+            )
+
+        q_bf = tile([P, Q, PACK], BF16, "q_bf")
+        interleave("V", nc, q_bf[:], q_raw[:])
+        q_codes = tile([P, Q], U32, "q_codes")
+        q_scales = tile([P, Q], U8, "q_scales")
+        nc.vector.quantize_mx(out=q_codes[:].bitcast(FP8X4), scales=q_scales[:], in_=q_bf[:].rearrange("p q j -> p (q j)"))
+
+        a = tile([P, T], F32, "a")
+        half_max = [tile([P, 1], F32, f"half_max{g}") for g in range(PASSES)]
+        for g in range(PASSES):
+            bank = ps.tile([P, KP], F32, name=f"a_bank{g}")
+            nc.tensor.matmul_mx(
+                out=bank[:],
+                lhsT=q_codes[:].bitcast(FP8X4),
+                lhsT_scale=q_scales[:],
+                rhs=k_words[:, 2 * g * KP : 2 * (g + 1) * KP].bitcast(FP4X4),
+                rhs_scale=k_scales[:, g * KP : (g + 1) * KP],
+                start=True,
+                stop=True,
+            )
+            nc.vector.tensor_scalar(
+                out=a[:, g * KP : (g + 1) * KP], in0=bank[:], scalar1=1.0, scalar2=None,
+                op0=ALU.mult, op1=ALU.max, accum_out=half_max[g][:],
+            )
+        neg_max = tile([P, 1], F32, "neg_max")
+        nc.vector.tensor_scalar(
+            out=neg_max[:], in0=half_max[0][:], scalar1=half_max[1][:], scalar2=-1.0, op0=ALU.max, op1=ALU.mult
+        )
+        p = []
+        z_half = tile([P, PASSES], F32, "z_half")
+        pk = tile([P, I], F32, "pk")
+        sk = tile([P, 1], F32, "sk")
+        ak = tile([P, I], F32, "ak")
+        nc.vector.tensor_copy(out=ak[:], in_=a[:].indirect(offsets[:]))
+        for g in range(PASSES):
+            p.append(tile([P, KP], F32, f"p{g}", None))
+            nc.scalar.activation(
+                out=p[g][:], in_=a[:, g * KP : (g + 1) * KP], func=ACT.Exp,
+                bias=neg_max[:], accum_out=z_half[:, g : g + 1],
+            )
+            if g == 0:
+                nc.scalar.activation(out=pk[:], in_=ak[:], func=ACT.Exp, bias=neg_max[:], accum_out=sk[:])
+        cast(0, "S")
+        cast(1, "S")
+        cast(2, "V", "half_max0")
+        quant(0, "half_max1")
+        quant(1)
+        nc.vector.tensor_copy(out=pf[:].indirect(offsets[:]), in_=pk[:])
+        rest = tile([P, 1], F32, "rest")
+        nc.scalar.activation(out=rest[:], in_=z_half[:, 0:1], func=ACT.Identity, scale=-1.0, bias=sk[:])
+        zz = tile([P, 2], F32, "zz")
+        nc.scalar.activation(out=zz[:, 0:1], in_=z_half[:, 0:1], func=ACT.Identity, bias=z_half[:, 1:2])
+        nc.scalar.activation(out=zz[:, 1:2], in_=z_half[:, 1:2], func=ACT.Identity, scale=-1.0, bias=rest[:])
+        cast(3, "S", "rest")
+        cast(4, "S", "z_half")
+        cast(5, "S", "v_raw01")
+        cast(6, "S", "v_raw10")
+        cast(7, "S", "v_bf4x")
+        rz = tile([P, 2], F32, "rz")
+        nc.vector.reciprocal(out=rz[:], in_=zz[:])
+        c1 = tile([P, 1], F32, "c1")
+        nc.vector.tensor_scalar(
+            out=c1[:], in0=sk[:], scalar1=rz[:, 0:1], scalar2=rz[:, 1:2], op0=ALU.mult, op1=ALU.mult
+        )
+        quant(2, "zz")
+        p_scaled = []
+        for g in range(PASSES):
+            ps_t = tile([P, KP], F32, f"p_scaled{g}")
+            nc.vector.tensor_scalar(
+                out=ps_t[:], in0=pf[:, g * KP : (g + 1) * KP], scalar1=rz[:, 1:2], scalar2=-1.0, op0=ALU.mult, op1=ALU.mult
+            )
+            p_scaled.append(ps_t)
+        w_banks = []
+        us = []
+        for g in range(PASSES):
+            u = tile([P, PACK, P], F32, f"u{g}")
+            nc.vector.scalar_tensor_tensor(
+                out=u[:].rearrange("q j s -> q s j"),
+                in0=p[g][:].rearrange("q (s j) -> q s j", j=PACK),
+                scalar=c1[:],
+                in1=p_scaled[g][:].rearrange("q (s j) -> q s j", j=PACK),
+                op0=ALU.mult, op1=ALU.add,
+            )
+            us.append(u)
+            w_bank = ps.tile([P, PACK, Q], F32, name=f"w_bank{g}")
+            for j in range(PACK):
+                nc.tensor.transpose(w_bank[:, j, :], u[:, j, :], ident[:])
+            w_banks.append(w_bank)
+        w_bfs = []
+        w_q = []
+
+        def weigh(g):
+            w_bf = tile([P, Q, PACK], BF16, f"w_bf{g}")
+            nc.vector.tensor_tensor(
+                out=w_bf[:], in0=w_banks[g][:].rearrange("p j q -> p q j"),
+                in1=fac_t[:, g : g + 1, :].to_broadcast([P, Q, PACK]), op=ALU.mult,
+            )
+            w_bfs.append(w_bf)
+
+        def quant_w(g):
+            w_codes = tile([P, Q], U32, f"w_codes{g}")
+            w_scales = tile([P, Q], U8, f"w_scales{g}")
+            nc.vector.quantize_mx(out=w_codes[:].bitcast(FP8X4), scales=w_scales[:], in_=w_bfs[g][:].rearrange("p q j -> p (q j)"))
+            w_q.append((w_codes, w_scales))
+
+        weigh(0)
+        quant_w(0)
+        weigh(1)
+        quant_w(1)
+        for piece in range(3, 8):
+            quant(piece)
+
+        o_banks = [ps.tile([P, HALF], F32, name=f"o_bank{h}") for h in range(2)]
+        for g in range(PASSES):
+            for h in range(2):
+                nc.tensor.matmul_mx(
+                    out=o_banks[h][:],
+                    lhsT=w_q[g][0][:].bitcast(FP8X4),
+                    lhsT_scale=w_q[g][1][:],
+                    rhs=v_codes[g, h][:].bitcast(FP8X4),
+                    rhs_scale=v_scales[g, h][:],
+                    start=(g == 0),
+                    stop=(g == PASSES - 1),
+                )
+        for h in range(2):
+            o_sb = tile([P, HALF], F32, f"o_sb{h}")
+            if h == 0:
+                nc.scalar.copy(out=o_sb[:], in_=o_banks[h][:])
+                nc.scalar.dma_start(out=out[:, h * HALF : (h + 1) * HALF], in_=o_sb[:])
+            else:
+                nc.vector.tensor_copy(out=o_sb[:], in_=o_banks[h][:])
+                nc.sync.dma_start(out=out[:, h * HALF : (h + 1) * HALF], in_=o_sb[:])

@@ -16,7 +16,6 @@ FP8X4 = mybir.dt.float8_e4m3fn_x4
 FP4X4 = mybir.dt.float4_e2m1fn_x4
 ALU = mybir.AluOpType
 ACT = mybir.ActivationFunctionType
-AX = mybir.AxisListType
 
 P = 128
 PACK = 4
@@ -24,6 +23,7 @@ KP = P * PACK
 PASSES = T // KP
 HALF = E // 2
 PIECE = 128
+QV = 80
 
 
 def interleave(eng, nc, dst, src):
@@ -31,6 +31,8 @@ def interleave(eng, nc, dst, src):
     s = src.rearrange("p t (c i) -> p c t i", i=4)
     if eng == "S":
         nc.scalar.copy(out=d, in_=s)
+    elif eng == "A":
+        nc.scalar.activation(out=d, in_=s, func=ACT.Copy)
     elif eng == "V":
         nc.vector.tensor_copy(out=d, in_=s)
     else:
@@ -49,10 +51,6 @@ def tile_attend_knockout_heads_kernel(tc, query, keys_words, keys_scales, fac, v
         offsets = sb.tile([P, I // 16], U16, name="offsets")
         k_scales = tile([P, T], U8, "k_scales")
         nc.vector.memset(k_scales[:].bitcast(I32), 0)
-        warm_in = tile([P, 1], F32, "warm_in")
-        nc.vector.memset(warm_in[:], 0.0)
-        warm_out = tile([P, 1], F32, "warm_out")
-        nc.scalar.activation(out=warm_out[:], in_=warm_in[:], func=ACT.Exp)
 
         q_raw = tile([P, PACK, Q], F32, "q_raw")
         nc.sync.dma_start(out=q_raw[:], in_=query.rearrange("(p j) q -> p j q", j=PACK))
@@ -72,8 +70,8 @@ def tile_attend_knockout_heads_kernel(tc, query, keys_words, keys_scales, fac, v
             v_raw[g, h] = t
 
         load_vals(0, 0)
-        load_vals(0, 1)
         nc.sync.dma_start(offsets[:], offs)
+        load_vals(0, 1)
         load_vals(1, 0)
         load_vals(1, 1)
         fac_t = tile([P, PASSES, PACK], F32, "fac_t")
@@ -109,7 +107,8 @@ def tile_attend_knockout_heads_kernel(tc, query, keys_words, keys_scales, fac, v
             )
 
         q_bf = tile([P, Q, PACK], BF16, "q_bf")
-        interleave("V", nc, q_bf[:], q_raw[:])
+        interleave("V", nc, q_bf[:, 0:QV, :], q_raw[:, :, 0:QV])
+        interleave("A", nc, q_bf[:, QV:Q, :], q_raw[:, :, QV:Q])
         q_codes = tile([P, Q], U32, "q_codes")
         q_scales = tile([P, Q], U8, "q_scales")
         nc.vector.quantize_mx(out=q_codes[:].bitcast(FP8X4), scales=q_scales[:], in_=q_bf[:].rearrange("p q j -> p (q j)"))
@@ -135,20 +134,24 @@ def tile_attend_knockout_heads_kernel(tc, query, keys_words, keys_scales, fac, v
         nc.vector.tensor_scalar(
             out=neg_max[:], in0=half_max[0][:], scalar1=half_max[1][:], scalar2=-1.0, op0=ALU.max, op1=ALU.mult
         )
-        p = []
+        p = [tile([P, PACK, P], F32, f"p{g}") for g in range(PASSES)]
         z_half = tile([P, PASSES], F32, "z_half")
         pk = tile([P, I], F32, "pk")
         sk = tile([P, 1], F32, "sk")
+
+        def exp_half(g):
+            nc.scalar.activation(
+                out=p[g][:].rearrange("q j s -> q s j"),
+                in_=a[:, g * KP : (g + 1) * KP].rearrange("q (s j) -> q s j", j=PACK),
+                func=ACT.Exp, bias=neg_max[:], accum_out=z_half[:, g : g + 1],
+            )
+
         ak = tile([P, I], F32, "ak")
         nc.vector.tensor_copy(out=ak[:], in_=a[:].indirect(offsets[:]))
-        for g in range(PASSES):
-            p.append(tile([P, KP], F32, f"p{g}", None))
-            nc.scalar.activation(
-                out=p[g][:], in_=a[:, g * KP : (g + 1) * KP], func=ACT.Exp,
-                bias=neg_max[:], accum_out=z_half[:, g : g + 1],
-            )
-            if g == 0:
-                nc.scalar.activation(out=pk[:], in_=ak[:], func=ACT.Exp, bias=neg_max[:], accum_out=sk[:])
+        exp_half(0)
+        nc.scalar.activation(out=pk[:], in_=ak[:], func=ACT.Exp, bias=neg_max[:], accum_out=sk[:])
+        exp_half(1)
+
         cast(0, "S")
         cast(1, "S")
         cast(2, "V", "half_max0")
@@ -157,85 +160,100 @@ def tile_attend_knockout_heads_kernel(tc, query, keys_words, keys_scales, fac, v
         nc.vector.tensor_copy(out=pf[:].indirect(offsets[:]), in_=pk[:])
         rest = tile([P, 1], F32, "rest")
         nc.scalar.activation(out=rest[:], in_=z_half[:, 0:1], func=ACT.Identity, scale=-1.0, bias=sk[:])
-        zz = tile([P, 2], F32, "zz")
+        zz = tile([P, 3], F32, "zz")
         nc.scalar.activation(out=zz[:, 0:1], in_=z_half[:, 0:1], func=ACT.Identity, bias=z_half[:, 1:2])
         nc.scalar.activation(out=zz[:, 1:2], in_=z_half[:, 1:2], func=ACT.Identity, scale=-1.0, bias=rest[:])
-        cast(3, "S", "rest")
-        cast(4, "S", "z_half")
-        cast(5, "S", "v_raw01")
-        cast(6, "S", "v_raw10")
-        cast(7, "S", "v_bf4x")
-        rz = tile([P, 2], F32, "rz")
+        nc.scalar.activation(out=zz[:, 2:3], in_=rest[:], func=ACT.Identity, scale=-1.0, bias=z_half[:, 1:2])
+        rz = tile([P, 3], F32, "rz")
         nc.vector.reciprocal(out=rz[:], in_=zz[:])
+        pf_second = tile([P, PACK, P], F32, "pf_second")
+
+        pf_first = [tile([P, 2, P], F32, f"pf_first{i}") for i in range(2)]
+
+        def scale_pf(i):
+            nc.vector.tensor_scalar(
+                out=pf_first[i][:].rearrange("q j s -> q s j"),
+                in0=pf[:, 0:KP].rearrange("q (s j) -> q s j", j=PACK)[:, :, 2 * i : 2 * i + 2],
+                scalar1=rz[:, 2:3], scalar2=None, op0=ALU.mult,
+            )
+
         c1 = tile([P, 1], F32, "c1")
         nc.vector.tensor_scalar(
             out=c1[:], in0=sk[:], scalar1=rz[:, 0:1], scalar2=rz[:, 1:2], op0=ALU.mult, op1=ALU.mult
         )
+        scale_pf(0)
+        scale_pf(1)
+        nc.scalar.activation(
+            out=pf_second[:].rearrange("q j s -> q s j"),
+            in_=pf[:, KP:T].rearrange("q (s j) -> q s j", j=PACK), func=ACT.Copy, scale=rz[:, 2:3],
+        )
         quant(2, "zz")
-        p_scaled = []
-        for g in range(PASSES):
-            ps_t = tile([P, KP], F32, f"p_scaled{g}")
-            nc.vector.tensor_scalar(
-                out=ps_t[:], in0=pf[:, g * KP : (g + 1) * KP], scalar1=rz[:, 1:2], scalar2=-1.0, op0=ALU.mult, op1=ALU.mult
-            )
-            p_scaled.append(ps_t)
+        cast(3, "S", "rest")
+        cast(4, "S", "z_half")
+        cast(5, "S")
+        cast(6, "S")
+        cast(7, "S")
         w_banks = []
         us = []
         for g in range(PASSES):
-            u = tile([P, PACK, P], F32, f"u{g}")
-            nc.vector.scalar_tensor_tensor(
-                out=u[:].rearrange("q j s -> q s j"),
-                in0=p[g][:].rearrange("q (s j) -> q s j", j=PACK),
-                scalar=c1[:],
-                in1=p_scaled[g][:].rearrange("q (s j) -> q s j", j=PACK),
-                op0=ALU.mult, op1=ALU.add,
-            )
-            us.append(u)
             w_bank = ps.tile([P, PACK, Q], F32, name=f"w_bank{g}")
-            for j in range(PACK):
-                nc.tensor.transpose(w_bank[:, j, :], u[:, j, :], ident[:])
+            step = 2
+            for j0 in range(0, PACK, step):
+                u = tile([P, step, P], F32, f"u{g}{j0}")
+                nc.vector.scalar_tensor_tensor(
+                    out=u[:], in0=p[g][:, j0 : j0 + step, :], scalar=c1[:], in1=pf_first[j0 // 2][:] if g == 0 else pf_second[:, j0 : j0 + step, :],
+                    op0=ALU.mult, op1=ALU.add,
+                )
+                us.append(u)
+                for j in range(step):
+                    nc.tensor.transpose(w_bank[:, j0 + j, :], u[:, j, :], ident[:])
             w_banks.append(w_bank)
-        w_bfs = []
-        w_q = []
+        w_bfs = [tile([P, Q, PACK], BF16, f"w_bf{g}") for g in range(PASSES)]
+        w_codes = [tile([P, Q], U32, f"w_codes{g}") for g in range(PASSES)]
+        w_scales = [tile([P, Q], U8, f"w_scales{g}") for g in range(PASSES)]
 
-        def weigh(g):
-            w_bf = tile([P, Q, PACK], BF16, f"w_bf{g}")
+        def weigh(g, q0, q1):
             nc.vector.tensor_tensor(
-                out=w_bf[:], in0=w_banks[g][:].rearrange("p j q -> p q j"),
-                in1=fac_t[:, g : g + 1, :].to_broadcast([P, Q, PACK]), op=ALU.mult,
+                out=w_bfs[g][:, q0:q1, :], in0=w_banks[g][:, :, q0:q1].rearrange("p j q -> p q j"),
+                in1=fac_t[:, g : g + 1, :].to_broadcast([P, q1 - q0, PACK]), op=ALU.mult,
             )
-            w_bfs.append(w_bf)
 
-        def quant_w(g):
-            w_codes = tile([P, Q], U32, f"w_codes{g}")
-            w_scales = tile([P, Q], U8, f"w_scales{g}")
-            nc.vector.quantize_mx(out=w_codes[:].bitcast(FP8X4), scales=w_scales[:], in_=w_bfs[g][:].rearrange("p q j -> p (q j)"))
-            w_q.append((w_codes, w_scales))
+        def quant_w(g, q0, q1):
+            nc.vector.quantize_mx(
+                out=w_codes[g][:, q0:q1].bitcast(FP8X4), scales=w_scales[g][:, q0:q1],
+                in_=w_bfs[g][:, q0:q1, :].rearrange("p q j -> p (q j)"),
+            )
 
-        weigh(0)
-        quant_w(0)
-        weigh(1)
-        quant_w(1)
-        for piece in range(3, 8):
+        weigh(0, 0, Q)
+        quant_w(0, 0, Q)
+        weigh(1, 0, Q // 2)
+        weigh(1, Q // 2, Q)
+        quant_w(1, 0, Q // 2)
+        quant_w(1, Q // 2, Q)
+        for piece in range(3, 6):
             quant(piece)
+        quant(6, "fac_t")
+        quant(7)
 
-        o_banks = [ps.tile([P, HALF], F32, name=f"o_bank{h}") for h in range(2)]
+        parts = [(0, 256), (256, 384), (384, 512)]
+        o_banks = [ps.tile([P, e1 - e0], F32, name=f"o_bank{e0}") for e0, e1 in parts]
         for g in range(PASSES):
-            for h in range(2):
+            for bank, (e0, e1) in zip(o_banks, parts):
+                h, cols = e0 // HALF, slice(e0 % HALF, e0 % HALF + e1 - e0)
                 nc.tensor.matmul_mx(
-                    out=o_banks[h][:],
-                    lhsT=w_q[g][0][:].bitcast(FP8X4),
-                    lhsT_scale=w_q[g][1][:],
-                    rhs=v_codes[g, h][:].bitcast(FP8X4),
-                    rhs_scale=v_scales[g, h][:],
+                    out=bank[:],
+                    lhsT=w_codes[g][:].bitcast(FP8X4),
+                    lhsT_scale=w_scales[g][:],
+                    rhs=v_codes[g, h][:, cols].bitcast(FP8X4),
+                    rhs_scale=v_scales[g, h][:, cols],
                     start=(g == 0),
                     stop=(g == PASSES - 1),
                 )
-        for h in range(2):
-            o_sb = tile([P, HALF], F32, f"o_sb{h}")
-            if h == 0:
-                nc.scalar.copy(out=o_sb[:], in_=o_banks[h][:])
-                nc.scalar.dma_start(out=out[:, h * HALF : (h + 1) * HALF], in_=o_sb[:])
+        for bank, (e0, e1) in zip(o_banks, parts):
+            o_sb = tile([P, e1 - e0], F32, f"o_sb{e0}")
+            if e0 == 0:
+                nc.scalar.copy(out=o_sb[:], in_=bank[:])
+                nc.scalar.dma_start(out=out[:, e0:e1], in_=o_sb[:])
             else:
-                nc.vector.tensor_copy(out=o_sb[:], in_=o_banks[h][:])
-                nc.sync.dma_start(out=out[:, h * HALF : (h + 1) * HALF], in_=o_sb[:])
+                nc.vector.tensor_copy(out=o_sb[:], in_=bank[:])
+                nc.sync.dma_start(out=out[:, e0:e1], in_=o_sb[:])

@@ -114,36 +114,39 @@ def tile_attend_knockout_heads_kernel(tc, query, keys_words, keys_scales, fac, v
         nc.vector.quantize_mx(out=q_codes[:].bitcast(FP8X4), scales=q_scales[:], in_=q_bf[:].rearrange("p q j -> p (q j)"))
 
         a = tile([P, T], F32, "a")
-        half_max = [tile([P, 1], F32, f"half_max{g}") for g in range(PASSES)]
-        for g in range(PASSES):
-            bank = ps.tile([P, KP], F32, name=f"a_bank{g}")
+        run_max = [tile([P, 1], F32, f"half_max{i}") for i in range(4)]
+        for i in range(4):
+            bank = ps.tile([P, 256], F32, name=f"a_bank{i}", tag=f"bank{i}")
             nc.tensor.matmul_mx(
                 out=bank[:],
                 lhsT=q_codes[:].bitcast(FP8X4),
                 lhsT_scale=q_scales[:],
-                rhs=k_words[:, 2 * g * KP : 2 * (g + 1) * KP].bitcast(FP4X4),
-                rhs_scale=k_scales[:, g * KP : (g + 1) * KP],
+                rhs=k_words[:, 512 * i : 512 * (i + 1)].bitcast(FP4X4),
+                rhs_scale=k_scales[:, 256 * i : 256 * (i + 1)],
                 start=True,
                 stop=True,
             )
             nc.vector.tensor_scalar(
-                out=a[:, g * KP : (g + 1) * KP], in0=bank[:], scalar1=1.0, scalar2=None,
-                op0=ALU.mult, op1=ALU.max, accum_out=half_max[g][:],
+                out=a[:, 256 * i : 256 * (i + 1)], in0=bank[:], scalar1=1.0,
+                scalar2=run_max[i - 2][:] if i >= 2 else None,
+                op0=ALU.mult, op1=ALU.max, accum_out=run_max[i][:],
             )
         neg_max = tile([P, 1], F32, "neg_max")
         nc.vector.tensor_scalar(
-            out=neg_max[:], in0=half_max[0][:], scalar1=half_max[1][:], scalar2=-1.0, op0=ALU.max, op1=ALU.mult
+            out=neg_max[:], in0=run_max[2][:], scalar1=run_max[3][:], scalar2=-1.0, op0=ALU.max, op1=ALU.mult
         )
-        p = [tile([P, PACK, P], F32, f"p{g}") for g in range(PASSES)]
-        z_half = tile([P, PASSES], F32, "z_half")
+        p = tile([P, PACK, T // PACK], F32, "p")
+        cuts = [0, 112, T // PACK]
+        z_first = tile([P, 2], F32, "z_first")
+        z_second = tile([P, 1], F32, "z_second")
         pk = tile([P, I], F32, "pk")
         sk = tile([P, 1], F32, "sk")
 
         def exp_half(g):
             nc.scalar.activation(
-                out=p[g][:].rearrange("q j s -> q s j"),
-                in_=a[:, g * KP : (g + 1) * KP].rearrange("q (s j) -> q s j", j=PACK),
-                func=ACT.Exp, bias=neg_max[:], accum_out=z_half[:, g : g + 1],
+                out=p[:, :, cuts[g] : cuts[g + 1]].rearrange("q j s -> q s j"),
+                in_=a[:, PACK * cuts[g] : PACK * cuts[g + 1]].rearrange("q (s j) -> q s j", j=PACK),
+                func=ACT.Exp, bias=neg_max[:], accum_out=(z_first[:, 0:1], z_second[:])[g],
             )
 
         ak = tile([P, I], F32, "ak")
@@ -154,17 +157,14 @@ def tile_attend_knockout_heads_kernel(tc, query, keys_words, keys_scales, fac, v
 
         cast(0, "S")
         cast(1, "S")
-        cast(2, "V", "half_max0")
-        quant(0, "half_max1")
+        cast(2, "V", "half_max2")
+        quant(0, "half_max3")
         quant(1)
         nc.vector.tensor_copy(out=pf[:].indirect(offsets[:]), in_=pk[:])
-        rest = tile([P, 1], F32, "rest")
-        nc.scalar.activation(out=rest[:], in_=z_half[:, 0:1], func=ACT.Identity, scale=-1.0, bias=sk[:])
-        zz = tile([P, 3], F32, "zz")
-        nc.scalar.activation(out=zz[:, 0:1], in_=z_half[:, 0:1], func=ACT.Identity, bias=z_half[:, 1:2])
-        nc.scalar.activation(out=zz[:, 1:2], in_=z_half[:, 1:2], func=ACT.Identity, scale=-1.0, bias=rest[:])
-        nc.scalar.activation(out=zz[:, 2:3], in_=rest[:], func=ACT.Identity, scale=-1.0, bias=z_half[:, 1:2])
-        rz = tile([P, 3], F32, "rz")
+        nc.scalar.activation(out=z_first[:, 1:2], in_=sk[:], func=ACT.Identity, scale=-1.0, bias=z_first[:, 0:1])
+        zz = tile([P, 2], F32, "zz")
+        nc.scalar.activation(out=zz[:], in_=z_first[:], func=ACT.Identity, bias=z_second[:])
+        rz = tile([P, 2], F32, "rz")
         nc.vector.reciprocal(out=rz[:], in_=zz[:])
         pf_second = tile([P, PACK, P], F32, "pf_second")
 
@@ -174,7 +174,7 @@ def tile_attend_knockout_heads_kernel(tc, query, keys_words, keys_scales, fac, v
             nc.vector.tensor_scalar(
                 out=pf_first[i][:].rearrange("q j s -> q s j"),
                 in0=pf[:, 0:KP].rearrange("q (s j) -> q s j", j=PACK)[:, :, 2 * i : 2 * i + 2],
-                scalar1=rz[:, 2:3], scalar2=None, op0=ALU.mult,
+                scalar1=rz[:, 1:2], scalar2=None, op0=ALU.mult,
             )
 
         c1 = tile([P, 1], F32, "c1")
@@ -185,11 +185,11 @@ def tile_attend_knockout_heads_kernel(tc, query, keys_words, keys_scales, fac, v
         scale_pf(1)
         nc.scalar.activation(
             out=pf_second[:].rearrange("q j s -> q s j"),
-            in_=pf[:, KP:T].rearrange("q (s j) -> q s j", j=PACK), func=ACT.Copy, scale=rz[:, 2:3],
+            in_=pf[:, KP:T].rearrange("q (s j) -> q s j", j=PACK), func=ACT.Copy, scale=rz[:, 1:2],
         )
         quant(2, "zz")
-        cast(3, "S", "rest")
-        cast(4, "S", "z_half")
+        cast(3, "S", "z_first")
+        cast(4, "S", "z_second")
         cast(5, "S")
         cast(6, "S")
         cast(7, "S")
@@ -201,8 +201,8 @@ def tile_attend_knockout_heads_kernel(tc, query, keys_words, keys_scales, fac, v
             for j0 in range(0, PACK, step):
                 u = tile([P, step, P], F32, f"u{g}{j0}")
                 nc.vector.scalar_tensor_tensor(
-                    out=u[:], in0=p[g][:, j0 : j0 + step, :], scalar=c1[:], in1=pf_first[j0 // 2][:] if g == 0 else pf_second[:, j0 : j0 + step, :],
-                    op0=ALU.mult, op1=ALU.add,
+                    out=u[:], in0=p[:, j0 : j0 + step, g * P : (g + 1) * P], scalar=c1[:], in1=pf_first[j0 // 2][:] if g == 0 else pf_second[:, j0 : j0 + step, :],
+                    op0=ALU.mult, op1=ALU.subtract,
                 )
                 us.append(u)
                 for j in range(step):
@@ -213,9 +213,9 @@ def tile_attend_knockout_heads_kernel(tc, query, keys_words, keys_scales, fac, v
         w_scales = [tile([P, Q], U8, f"w_scales{g}") for g in range(PASSES)]
 
         def weigh(g, q0, q1):
-            nc.vector.tensor_tensor(
-                out=w_bfs[g][:, q0:q1, :], in0=w_banks[g][:, :, q0:q1].rearrange("p j q -> p q j"),
-                in1=fac_t[:, g : g + 1, :].to_broadcast([P, q1 - q0, PACK]), op=ALU.mult,
+            nc.vector.scalar_tensor_tensor(
+                out=w_bfs[g][:, q0:q1, :], in0=w_banks[g][:, :, q0:q1].rearrange("p j q -> p q j"), scalar=-1.0,
+                in1=fac_t[:, g : g + 1, :].to_broadcast([P, q1 - q0, PACK]), op0=ALU.mult, op1=ALU.mult,
             )
 
         def quant_w(g, q0, q1):
@@ -236,7 +236,7 @@ def tile_attend_knockout_heads_kernel(tc, query, keys_words, keys_scales, fac, v
         quant(7)
 
         parts = [(0, 256), (256, 384), (384, 512)]
-        o_banks = [ps.tile([P, e1 - e0], F32, name=f"o_bank{e0}") for e0, e1 in parts]
+        o_banks = [ps.tile([P, e1 - e0], F32, name=f"o_bank{e0}", tag=f"bank{i}") for i, (e0, e1) in enumerate(parts)]
         for g in range(PASSES):
             for bank, (e0, e1) in zip(o_banks, parts):
                 h, cols = e0 // HALF, slice(e0 % HALF, e0 % HALF + e1 - e0)

from contextlib import ExitStack

import concourse.mybir as mybir
from concourse.masks import make_identity

D, T, Q, I, E = 512, 1024, 128, 256, 512
FLOPS = 2 * D * Q * T + 2 * T * Q * E

F32 = mybir.dt.float32
BF16 = mybir.dt.bfloat16
U32 = mybir.dt.uint32
I32 = mybir.dt.int32
U16 = mybir.dt.uint16
U8 = mybir.dt.uint8
FP8X4 = mybir.dt.float8_e4m3fn_x4
FP4X4 = mybir.dt.float4_e2m1fn_x4
ALU = mybir.AluOpType
ACT = mybir.ActivationFunctionType

P = 128
PACK = 4
KP = P * PACK
PASSES = T // KP
HALF = E // 2
PIECE = 128
QV = 80


def interleave(eng, nc, dst, src):
    d = dst.rearrange("p (c i) t -> p c t i", i=4)
    s = src.rearrange("p t (c i) -> p c t i", i=4)
    if eng == "S":
        nc.scalar.copy(out=d, in_=s)
    elif eng == "A":
        nc.scalar.activation(out=d, in_=s, func=ACT.Copy)
    elif eng == "V":
        nc.vector.tensor_copy(out=d, in_=s)
    else:
        nc.gpsimd.tensor_scalar(out=d, in0=s, scalar1=1.0, scalar2=0.0, op0=ALU.mult, op1=ALU.add)


def tile_attend_knockout_heads_kernel(tc, query, keys_words, keys_scales, fac, vals, offs, out):
    nc = tc.nc
    with ExitStack() as ctx:
        sb = ctx.enter_context(tc.tile_pool(name="sb", bufs=1))
        ps = ctx.enter_context(tc.psum_pool(name="ps", bufs=1))

        def tile(shape, dtype, name, tag=None):
            return sb.tile(shape, dtype, name=name, tag=tag or name, align_bytes=64)

        offsets = sb.tile([P, I // 16], U16, name="offsets")
        k_scales = tile([P, T], U8, "k_scales")
        nc.vector.memset(k_scales[:].bitcast(I32), 0)

        q_raw = tile([P, PACK, Q], F32, "q_raw")
        nc.sync.dma_start(out=q_raw[:], in_=query.rearrange("(p j) q -> p j q", j=PACK))
        k_words = tile([P, 2 * T], U8, "k_words")
        nc.sync.dma_start(out=k_words[:].bitcast(I32), in_=keys_words[0].bitcast(I32))
        for quad in range(4):
            nc.sync.dma_start(
                out=k_scales[32 * quad : 32 * quad + 4, :].bitcast(I32),
                in_=keys_scales[0, 4 * quad : 4 * quad + 4, :].bitcast(I32),
            )
        v_raw = {}

        def load_vals(g, h):
            t = tile([P, PACK, HALF], F32, f"v_raw{g}{h}")
            rows = vals[g * KP : (g + 1) * KP, h * HALF : (h + 1) * HALF]
            nc.sync.dma_start(out=t[:], in_=rows.rearrange("(p j) e -> p j e", j=PACK))
            v_raw[g, h] = t

        load_vals(0, 0)
        nc.sync.dma_start(offsets[:], offs)
        load_vals(0, 1)
        load_vals(1, 0)
        load_vals(1, 1)
        fac_t = tile([P, PASSES, PACK], F32, "fac_t")
        nc.sync.dma_start(out=fac_t[:], in_=fac[0].rearrange("(g p j) -> p g j", p=P, j=PACK))

        ident = tile([P, P], F32, "ident")
        make_identity(nc, ident[:])
        pf = tile([P, T], F32, "pf")
        nc.vector.memset(pf[:], 0.0)

        v_bf = {}
        v_codes = {}
        v_scales = {}

        def cast(piece, eng, tag=None):
            g, h, c0 = piece // 4, piece // 2 % 2, piece % 2 * PIECE
            if piece == 4:
                late = tile([P, 4, PIECE, PACK], BF16, "v_bf_late", tag)
                for i in range(4):
                    v_bf[4 + i] = late[:, i]
            elif piece < 4:
                v_bf[piece] = tile([P, PIECE, PACK], BF16, f"v_bf{piece}", tag)[:]
            interleave(eng, nc, v_bf[piece], v_raw[g, h][:, :, c0 : c0 + PIECE])

        def quant(piece, tag=None):
            g, h, c0 = piece // 4, piece // 2 % 2, piece % 2 * PIECE
            if (g, h) not in v_codes:
                v_codes[g, h] = tile([P, HALF], U32, f"v_codes{g}{h}", tag)
                v_scales[g, h] = tile([P, HALF], U8, f"v_scales{g}{h}")
            nc.vector.quantize_mx(
                out=v_codes[g, h][:, c0 : c0 + PIECE].bitcast(FP8X4), scales=v_scales[g, h][:, c0 : c0 + PIECE],
                in_=v_bf[piece].rearrange("p e j -> p (e j)"),
            )

        q_bf = tile([P, Q, PACK], BF16, "q_bf")
        interleave("V", nc, q_bf[:, 0:QV, :], q_raw[:, :, 0:QV])
        interleave("A", nc, q_bf[:, QV:Q, :], q_raw[:, :, QV:Q])
        q_codes = tile([P, Q], U32, "q_codes")
        q_scales = tile([P, Q], U8, "q_scales")
        nc.vector.quantize_mx(out=q_codes[:].bitcast(FP8X4), scales=q_scales[:], in_=q_bf[:].rearrange("p q j -> p (q j)"))

        a = tile([P, T], F32, "a")
        run_max = [tile([P, 1], F32, f"half_max{i}") for i in range(4)]
        for i in range(4):
            bank = ps.tile([P, 256], F32, name=f"a_bank{i}", tag=f"bank{i}")
            nc.tensor.matmul_mx(
                out=bank[:],
                lhsT=q_codes[:].bitcast(FP8X4),
                lhsT_scale=q_scales[:],
                rhs=k_words[:, 512 * i : 512 * (i + 1)].bitcast(FP4X4),
                rhs_scale=k_scales[:, 256 * i : 256 * (i + 1)],
                start=True,
                stop=True,
            )
            nc.vector.tensor_scalar(
                out=a[:, 256 * i : 256 * (i + 1)], in0=bank[:], scalar1=1.0,
                scalar2=run_max[i - 2][:] if i >= 2 else None,
                op0=ALU.mult, op1=ALU.max, accum_out=run_max[i][:],
            )
        neg_max = tile([P, 1], F32, "neg_max")
        nc.vector.tensor_scalar(
            out=neg_max[:], in0=run_max[2][:], scalar1=run_max[3][:], scalar2=-1.0, op0=ALU.max, op1=ALU.mult
        )
        p = tile([P, PACK, T // PACK], F32, "p")
        cuts = [0, 112, T // PACK]
        z_first = tile([P, 2], F32, "z_first")
        z_second = tile([P, 1], F32, "z_second")
        pk = tile([P, I], F32, "pk")
        sk = tile([P, 1], F32, "sk")

        def exp_half(g):
            nc.scalar.activation(
                out=p[:, :, cuts[g] : cuts[g + 1]].rearrange("q j s -> q s j"),
                in_=a[:, PACK * cuts[g] : PACK * cuts[g + 1]].rearrange("q (s j) -> q s j", j=PACK),
                func=ACT.Exp, bias=neg_max[:], accum_out=(z_first[:, 0:1], z_second[:])[g],
            )

        ak = tile([P, I], F32, "ak")
        nc.vector.tensor_copy(out=ak[:], in_=a[:].indirect(offsets[:]))
        exp_half(0)
        nc.scalar.activation(out=pk[:], in_=ak[:], func=ACT.Exp, bias=neg_max[:], accum_out=sk[:])
        exp_half(1)

        cast(0, "S")
        cast(1, "S")
        cast(2, "V", "half_max2")
        quant(0, "half_max3")
        quant(1)
        nc.vector.tensor_copy(out=pf[:].indirect(offsets[:]), in_=pk[:])
        nc.scalar.activation(out=z_first[:, 1:2], in_=sk[:], func=ACT.Identity, scale=-1.0, bias=z_first[:, 0:1])
        zz = tile([P, 2], F32, "zz")
        nc.scalar.activation(out=zz[:], in_=z_first[:], func=ACT.Identity, bias=z_second[:])
        rz = tile([P, 2], F32, "rz")
        nc.vector.reciprocal(out=rz[:], in_=zz[:])
        pf_second = tile([P, PACK, P], F32, "pf_second")

        pf_first = [tile([P, 2, P], F32, f"pf_first{i}") for i in range(2)]

        def scale_pf(i):
            nc.vector.tensor_scalar(
                out=pf_first[i][:].rearrange("q j s -> q s j"),
                in0=pf[:, 0:KP].rearrange("q (s j) -> q s j", j=PACK)[:, :, 2 * i : 2 * i + 2],
                scalar1=rz[:, 1:2], scalar2=None, op0=ALU.mult,
            )

        c1 = tile([P, 1], F32, "c1")
        nc.vector.tensor_scalar(
            out=c1[:], in0=sk[:], scalar1=rz[:, 0:1], scalar2=rz[:, 1:2], op0=ALU.mult, op1=ALU.mult
        )
        scale_pf(0)
        scale_pf(1)
        nc.scalar.activation(
            out=pf_second[:].rearrange("q j s -> q s j"),
            in_=pf[:, KP:T].rearrange("q (s j) -> q s j", j=PACK), func=ACT.Copy, scale=rz[:, 1:2],
        )
        quant(2, "zz")
        cast(3, "S", "z_first")
        cast(4, "S", "z_second")
        cast(5, "S")
        cast(6, "S")
        cast(7, "S")
        w_banks = []
        us = []
        for g in range(PASSES):
            w_bank = ps.tile([P, PACK, Q], F32, name=f"w_bank{g}")
            step = 2
            for j0 in range(0, PACK, step):
                u = tile([P, step, P], F32, f"u{g}{j0}")
                nc.vector.scalar_tensor_tensor(
                    out=u[:], in0=p[:, j0 : j0 + step, g * P : (g + 1) * P], scalar=c1[:], in1=pf_first[j0 // 2][:] if g == 0 else pf_second[:, j0 : j0 + step, :],
                    op0=ALU.mult, op1=ALU.subtract,
                )
                us.append(u)
                for j in range(step):
                    nc.tensor.transpose(w_bank[:, j0 + j, :], u[:, j, :], ident[:])
            w_banks.append(w_bank)
        w_bfs = [tile([P, Q, PACK], BF16, f"w_bf{g}") for g in range(PASSES)]
        w_codes = [tile([P, Q], U32, f"w_codes{g}") for g in range(PASSES)]
        w_scales = [tile([P, Q], U8, f"w_scales{g}") for g in range(PASSES)]

        def weigh(g, q0, q1):
            nc.vector.scalar_tensor_tensor(
                out=w_bfs[g][:, q0:q1, :], in0=w_banks[g][:, :, q0:q1].rearrange("p j q -> p q j"), scalar=-1.0,
                in1=fac_t[:, g : g + 1, :].to_broadcast([P, q1 - q0, PACK]), op0=ALU.mult, op1=ALU.mult,
            )

        def quant_w(g, q0, q1):
            nc.vector.quantize_mx(
                out=w_codes[g][:, q0:q1].bitcast(FP8X4), scales=w_scales[g][:, q0:q1],
                in_=w_bfs[g][:, q0:q1, :].rearrange("p q j -> p (q j)"),
            )

        weigh(0, 0, Q)
        quant_w(0, 0, Q)
        weigh(1, 0, Q // 2)
        weigh(1, Q // 2, Q)
        quant_w(1, 0, Q // 2)
        quant_w(1, Q // 2, Q)
        for piece in range(3, 6):
            quant(piece)
        quant(6, "fac_t")
        quant(7)

        parts = [(0, 256), (256, 384), (384, 512)]
        o_banks = [ps.tile([P, e1 - e0], F32, name=f"o_bank{e0}", tag=f"bank{i}") for i, (e0, e1) in enumerate(parts)]
        for g in range(PASSES):
            for bank, (e0, e1) in zip(o_banks, parts):
                h, cols = e0 // HALF, slice(e0 % HALF, e0 % HALF + e1 - e0)
                nc.tensor.matmul_mx(
                    out=bank[:],
                    lhsT=w_codes[g][:].bitcast(FP8X4),
                    lhsT_scale=w_scales[g][:],
                    rhs=v_codes[g, h][:, cols].bitcast(FP8X4),
                    rhs_scale=v_scales[g, h][:, cols],
                    start=(g == 0),
                    stop=(g == PASSES - 1),
                )
        for bank, (e0, e1) in zip(o_banks, parts):
            o_sb = tile([P, e1 - e0], F32, f"o_sb{e0}")
            if e0 == 0:
                nc.scalar.copy(out=o_sb[:], in_=bank[:])
                nc.scalar.dma_start(out=out[:, e0:e1], in_=o_sb[:])
            else:
                nc.vector.tensor_copy(out=o_sb[:], in_=bank[:])
                nc.sync.dma_start(out=out[:, e0:e1], in_=o_sb[:])
